import numpy as np
import ml_dtypes

BF16 = ml_dtypes.bfloat16


def bf(x):
    return np.asarray(x, np.float32).astype(BF16)


def f32(x):
    return np.asarray(x, np.float32)


def f64(x):
    return np.asarray(x).astype(np.float64)


def striped(idx):
    return np.tile(idx.reshape(-1, 16).T, (8, 1))


S, K, M, N, E, Q, V, D = 512, 128, 512, 192, 2, 96, 256, 2


def setup_inputs():
    return {"base": bf(np.random.standard_normal((M, S))), "x": bf(np.random.standard_normal((K, N))), "w": bf(1.5 * np.random.standard_normal((E, K, M)) / np.sqrt(K)), "b": f32(0.5 * np.random.standard_normal((M, 1))), "offs": striped(np.random.permutation(S)[:N])}


def reference(base, x, w, b, offs):
    idx = offs[:16].T.reshape(-1)
    z = f64(base).copy()
    for e in range(E):
        z[:, idx[e * Q : (e + 1) * Q]] += f64(w)[e].T @ f64(x)[:, e * Q : (e + 1) * Q]
    z = np.maximum(z + f64(b), 0.0)
    return z.reshape(M, V, D).mean(axis=2)

@@ -1,0 +1,62 @@
+import concourse.mybir as mybir
+from concourse.masks import make_identity
+
+BF16, F32, U16 = mybir.dt.bfloat16, mybir.dt.float32, mybir.dt.uint16
+RELU = mybir.ActivationFunctionType.Relu
+ADD = mybir.AluOpType.add
+
+P = 128
+M, S, K, N, E = 512, 512, 128, 192, 2
+BLOCKS = M // P
+Q = N // E
+QC = Q // 16
+V = S // 2
+
+FLOPS = 2 * K * M * N + 4 * M * S
+
+
+def tile_rows_unpool_mean_relu_kernel(tc, base, x, w, b, offs, out):
+    nc = tc.nc
+    with (
+        tc.tile_pool(name="held", bufs=1) as held,
+        tc.psum_pool(name="windows", bufs=1) as windows,
+    ):
+        base_rows = [held.tile([P, S], BF16, name=f"base{a}") for a in range(BLOCKS)]
+        for a in range(BLOCKS):
+            nc.sync.dma_start(base_rows[a][:], base[a * P : (a + 1) * P, :])
+        points = held.tile([P, N], BF16, name="points")
+        nc.scalar.dma_start(points[:], x)
+        weights = held.tile([P, E, M], BF16, name="weights")
+        nc.scalar.dma_start(weights[:], w.rearrange("e k m -> k e m"))
+        offsets = held.tile([P, N // 16], U16, name="offsets")
+        nc.sync.dma_start(offsets[:], offs)
+        bias = held.tile([P, BLOCKS], F32, name="bias")
+        nc.scalar.dma_start(bias[:], b.rearrange("(a p) o -> p (a o)", p=P))
+        half_bias = held.tile([P, BLOCKS], F32, name="half_bias")
+        nc.vector.tensor_scalar_mul(half_bias[:], bias[:], 0.5)
+
+        identity = held.tile([P, P], BF16, name="identity")
+        make_identity(nc, identity[:])
+
+        window = [windows.tile([P, S], F32, name=f"window{a}") for a in range(BLOCKS)]
+        for a in range(BLOCKS):
+            nc.tensor.matmul(window[a][:], identity[:], base_rows[a][:], start=True, stop=False)
+
+        for a in range(BLOCKS):
+            for e in range(E):
+                nc.tensor.matmul(
+                    window[a][:].indirect(offsets[:, e * QC : (e + 1) * QC]),
+                    weights[:, e, a * P : (a + 1) * P],
+                    points[:, e * Q : (e + 1) * Q],
+                    start=False,
+                    stop=(e == E - 1),
+                )
+
+        for a in range(BLOCKS):
+            halves = held.tile([P, V, 2], F32, name=f"halves{a}")
+            nc.scalar.activation(
+                halves[:].rearrange("p v d -> p (v d)"), window[a][:], RELU, bias=half_bias[:, a : a + 1], scale=0.5
+            )
+            pooled = held.tile([P, V], F32, name=f"pooled{a}")
+            nc.vector.tensor_tensor(pooled[:], halves[:, :, 0], halves[:, :, 1], ADD)
+            nc.sync.dma_start(out[a * P : (a + 1) * P, :], pooled[:])

@@ -3,7 +3,7 @@ from concourse.masks import make_identity
 
 BF16, F32, U16 = mybir.dt.bfloat16, mybir.dt.float32, mybir.dt.uint16
 RELU = mybir.ActivationFunctionType.Relu
-ADD = mybir.AluOpType.add
+ADD, MULT, MAX = mybir.AluOpType.add, mybir.AluOpType.mult, mybir.AluOpType.max
 
 P = 128
 M, S, K, N, E = 512, 512, 128, 192, 2
@@ -34,6 +34,13 @@ def tile_rows_unpool_mean_relu_kernel(tc, base, x, w, b, offs, out):
         nc.scalar.dma_start(bias[:], b.rearrange("(a p) o -> p (a o)", p=P))
         half_bias = held.tile([P, BLOCKS], F32, name="half_bias")
         nc.vector.tensor_scalar_mul(half_bias[:], bias[:], 0.5)
+        minus_bias = held.tile([P, BLOCKS], F32, name="minus_bias")
+        nc.vector.tensor_scalar_mul(minus_bias[:], bias[:], -1.0)
+
+        zeros = held.tile([P, 1], F32, name="zeros")
+        nc.gpsimd.memset(zeros[:], 0.0)
+        early = held.tile([P, 1], F32, name="early")
+        nc.scalar.activation(early[:], zeros[:], RELU, bias=zeros[:])
 
         identity = held.tile([P, P], BF16, name="identity")
         make_identity(nc, identity[:])
@@ -54,9 +61,14 @@ def tile_rows_unpool_mean_relu_kernel(tc, base, x, w, b, offs, out):
 
         for a in range(BLOCKS):
             halves = held.tile([P, V, 2], F32, name=f"halves{a}")
-            nc.scalar.activation(
-                halves[:].rearrange("p v d -> p (v d)"), window[a][:], RELU, bias=half_bias[:, a : a + 1], scale=0.5
-            )
+            flat = halves[:].rearrange("p v d -> p (v d)")
             pooled = held.tile([P, V], F32, name=f"pooled{a}")
-            nc.vector.tensor_tensor(pooled[:], halves[:, :, 0], halves[:, :, 1], ADD)
+            if a % 2 == 0:
+                nc.scalar.activation(flat, window[a][:], RELU, bias=half_bias[:, a : a + 1], scale=0.5)
+                nc.gpsimd.tensor_tensor(pooled[:], halves[:, :, 0], halves[:, :, 1], ADD)
+            else:
+                nc.vector.tensor_scalar(flat, window[a][:], minus_bias[:, a : a + 1], 0.5, MAX, MULT)
+                nc.vector.scalar_tensor_tensor(
+                    pooled[:], halves[:, :, 0], bias[:, a : a + 1], halves[:, :, 1], ADD, ADD
+                )
             nc.sync.dma_start(out[a * P : (a + 1) * P, :], pooled[:])

@@ -25,13 +25,13 @@ def tile_rows_unpool_mean_relu_kernel(tc, base, x, w, b, offs, out):
         for a in range(BLOCKS):
             nc.sync.dma_start(base_rows[a][:], base[a * P : (a + 1) * P, :])
         points = held.tile([P, N], BF16, name="points")
-        nc.scalar.dma_start(points[:], x)
-        weights = held.tile([P, E, M], BF16, name="weights")
-        nc.scalar.dma_start(weights[:], w.rearrange("e k m -> k e m"))
+        nc.sync.dma_start(points[:], x)
         offsets = held.tile([P, N // 16], U16, name="offsets")
         nc.sync.dma_start(offsets[:], offs)
+        weights = held.tile([P, E, M], BF16, name="weights")
+        nc.sync.dma_start(weights[:], w.rearrange("e k m -> k e m"))
         bias = held.tile([P, BLOCKS], F32, name="bias")
-        nc.scalar.dma_start(bias[:], b.rearrange("(a p) o -> p (a o)", p=P))
+        nc.sync.dma_start(bias[:], b.rearrange("(a p) o -> p (a o)", p=P))
         half_bias = held.tile([P, BLOCKS], F32, name="half_bias")
         nc.vector.tensor_scalar_mul(half_bias[:], bias[:], 0.5)
         minus_bias = held.tile([P, BLOCKS], F32, name="minus_bias")

import concourse.mybir as mybir
from concourse.masks import make_identity

BF16, F32, U16 = mybir.dt.bfloat16, mybir.dt.float32, mybir.dt.uint16
RELU = mybir.ActivationFunctionType.Relu
ADD, MULT, MAX = mybir.AluOpType.add, mybir.AluOpType.mult, mybir.AluOpType.max

P = 128
M, S, K, N, E = 512, 512, 128, 192, 2
BLOCKS = M // P
Q = N // E
QC = Q // 16
V = S // 2

FLOPS = 2 * K * M * N + 4 * M * S


def tile_rows_unpool_mean_relu_kernel(tc, base, x, w, b, offs, out):
    nc = tc.nc
    with (
        tc.tile_pool(name="held", bufs=1) as held,
        tc.psum_pool(name="windows", bufs=1) as windows,
    ):
        base_rows = [held.tile([P, S], BF16, name=f"base{a}") for a in range(BLOCKS)]
        for a in range(BLOCKS):
            nc.sync.dma_start(base_rows[a][:], base[a * P : (a + 1) * P, :])
        points = held.tile([P, N], BF16, name="points")
        nc.sync.dma_start(points[:], x)
        offsets = held.tile([P, N // 16], U16, name="offsets")
        nc.sync.dma_start(offsets[:], offs)
        weights = held.tile([P, E, M], BF16, name="weights")
        nc.sync.dma_start(weights[:], w.rearrange("e k m -> k e m"))
        bias = held.tile([P, BLOCKS], F32, name="bias")
        nc.sync.dma_start(bias[:], b.rearrange("(a p) o -> p (a o)", p=P))
        half_bias = held.tile([P, BLOCKS], F32, name="half_bias")
        nc.vector.tensor_scalar_mul(half_bias[:], bias[:], 0.5)
        minus_bias = held.tile([P, BLOCKS], F32, name="minus_bias")
        nc.vector.tensor_scalar_mul(minus_bias[:], bias[:], -1.0)

        zeros = held.tile([P, 1], F32, name="zeros")
        nc.gpsimd.memset(zeros[:], 0.0)
        early = held.tile([P, 1], F32, name="early")
        nc.scalar.activation(early[:], zeros[:], RELU, bias=zeros[:])

        identity = held.tile([P, P], BF16, name="identity")
        make_identity(nc, identity[:])

        window = [windows.tile([P, S], F32, name=f"window{a}") for a in range(BLOCKS)]
        for a in range(BLOCKS):
            nc.tensor.matmul(window[a][:], identity[:], base_rows[a][:], start=True, stop=False)

        for a in range(BLOCKS):
            for e in range(E):
                nc.tensor.matmul(
                    window[a][:].indirect(offsets[:, e * QC : (e + 1) * QC]),
                    weights[:, e, a * P : (a + 1) * P],
                    points[:, e * Q : (e + 1) * Q],
                    start=False,
                    stop=(e == E - 1),
                )

        for a in range(BLOCKS):
            halves = held.tile([P, V, 2], F32, name=f"halves{a}")
            flat = halves[:].rearrange("p v d -> p (v d)")
            pooled = held.tile([P, V], F32, name=f"pooled{a}")
            if a % 2 == 0:
                nc.scalar.activation(flat, window[a][:], RELU, bias=half_bias[:, a : a + 1], scale=0.5)
                nc.gpsimd.tensor_tensor(pooled[:], halves[:, :, 0], halves[:, :, 1], ADD)
            else:
                nc.vector.tensor_scalar(flat, window[a][:], minus_bias[:, a : a + 1], 0.5, MAX, MULT)
                nc.vector.scalar_tensor_tensor(
                    pooled[:], halves[:, :, 0], bias[:, a : a + 1], halves[:, :, 1], ADD, ADD
                )
            nc.sync.dma_start(out[a * P : (a + 1) * P, :], pooled[:])
